import numpy as np
import ml_dtypes


def mxq(x, axis, fmt="e4m3"):
    dtype, down = {"e4m3": (ml_dtypes.float8_e4m3fn, 7), "e5m2": (ml_dtypes.float8_e5m2, 14)}[fmt]
    v = np.moveaxis(np.asarray(x, np.float32).astype(ml_dtypes.bfloat16).astype(np.float64), axis, -1)
    blocks = v.reshape(v.shape[:-1] + (-1, 32))
    amax = np.abs(blocks).max(-1, keepdims=True)
    byte = np.maximum(np.where(amax > 0, np.frexp(amax)[1] - 1 + 127, 0) - down, 1)
    scale = np.exp2(byte - 127.0)
    codes = (blocks / scale).astype(np.float32).astype(dtype).astype(np.float64)
    return np.moveaxis((codes * scale).reshape(v.shape), -1, axis)


WIDE = False


def mx_kscale(k):
    if not WIDE:
        return np.ones(k)
    levels = np.array([10, -10, 5, -5, 0])
    if k % 512:
        return np.exp2(np.random.permutation(np.resize(levels, k // 32))).repeat(32)
    a = np.empty((k // 512, 16))
    for p in range(k // 512):
        a[p, :8] = np.random.permutation(np.resize(levels, 8))
        for g in range(8):
            far = levels[np.abs(levels - a[p, g]) >= 10]
            a[p, g + 8] = far[np.random.randint(len(far))]
    return np.exp2(a.ravel()).repeat(32)


def f64(x):
    return np.asarray(x).astype(np.float64)


def striped(idx):
    return np.tile(idx.reshape(-1, 16).T, (8, 1)).astype(np.uint16)


def unstriped(offs):
    return offs[:16].T.reshape(-1).astype(np.int64)


E2M1 = np.array([0.0, 0.5, 1.0, 1.5, 2.0, 3.0, 4.0, 6.0, -0.0, -0.5, -1.0, -1.5, -2.0, -3.0, -4.0, -6.0])


def pack_weight(w, fmt):
    k, n = w.shape
    w = f64(np.asarray(w, np.float32).astype(ml_dtypes.bfloat16)).reshape(k // 32, 32, n)
    amax = np.abs(w).max(1)
    if fmt == "e4m3":
        byte = np.frexp(amax)[1] - 1 + 127 - 7
    else:
        mant, ex = np.frexp(amax / 6.0)
        byte = np.where(mant > 0.5, ex, ex - 1) + 127
    byte = np.clip(np.where(amax > 0, byte, 1), 1, 254)
    scaled = (w * np.exp2(127.0 - byte)[:, None, :]).reshape(k, n).astype(np.float32)
    by_word = np.ascontiguousarray(scaled.reshape(k // 512, 128, 4, n).transpose(0, 1, 3, 2))
    if fmt == "e4m3":
        words = by_word.astype(ml_dtypes.float8_e4m3fn).view(np.uint8)
    else:
        c = by_word.astype(ml_dtypes.float4_e2m1fn).view(np.uint8) & 0xF
        words = (c[..., 0::2] | (c[..., 1::2] << 4)).reshape(k // 512, 128, 2 * n)
    return np.ascontiguousarray(words), np.ascontiguousarray(byte.astype(np.uint8).reshape(k // 512, 16, n))


def unpack_weight(words, scales, fmt):
    g, _, n = scales.shape
    words = np.ascontiguousarray(words).reshape(g, 128, n, -1)
    if fmt == "e4m3":
        vals = words.view(ml_dtypes.float8_e4m3fn).astype(np.float64)
    else:
        nib = np.empty((g, 128, n, 4), np.uint8)
        nib[..., 0::2] = words & 0xF
        nib[..., 1::2] = words >> 4
        vals = E2M1[nib]
    vals = vals * np.repeat(np.exp2(scales.astype(np.float64) - 127.0), 8, axis=1)[..., None]
    return vals.transpose(0, 1, 3, 2).reshape(g * 512, n)


def gelu(v):
    return 0.5 * v * (1.0 + np.tanh(np.sqrt(2.0 / np.pi) * (v + 0.044715 * v**3)))


K, C, H, N, T, S = 1024, 512, 1024, 256, 2048, 1024

def setup_inputs():
    n = np.random.standard_normal
    s, sc, u = mx_kscale(K)[:, None], mx_kscale(C)[:, None], mx_kscale(H)[:, None]
    tab_words, tab_scales = pack_weight(n((K, T)) * s, "e4m3")
    tab2_words, tab2_scales = pack_weight(n((C, T)) * sc, "e4m3")
    wb_words, wb_scales = pack_weight(n((C, H)) / np.sqrt(C) / sc * u.T, "e2m1")
    return {
        "tab_words": tab_words, "tab_scales": tab_scales,
        "tab2_words": tab2_words, "tab2_scales": tab2_scales,
        "offs": striped(np.random.permutation(T)[:S]),
        "offs2": striped(np.random.permutation(T)[:S]),
        "wa": (n((K, H)) / np.sqrt(K) / s * u.T).astype(np.float32),
        "wb_words": wb_words, "wb_scales": wb_scales,
        "bh": (0.5 * n(H) * u[:, 0]).astype(np.float32),
        "wr": (n((H, N)) / np.sqrt(H) / u).astype(np.float32),
        "br": (0.5 * n(N)).astype(np.float32),
        "gT": n((N, T)).astype(np.float32),
    }

def reference(tab_words, tab_scales, tab2_words, tab2_scales, offs, offs2, wa, wb_words, wb_scales, bh, wr, br, gT):
    v = unpack_weight(tab_words, tab_scales, "e4m3")[:, unstriped(offs)]
    v2 = unpack_weight(tab2_words, tab2_scales, "e4m3")[:, unstriped(offs2)]
    g = f64(gT)[:, unstriped(offs)]
    a = mxq(f64(wa), 0, "e4m3")
    b = unpack_weight(wb_words, wb_scales, "e2m1")
    z = a.T @ v + b.T @ v2
    h = np.maximum(z + f64(bh)[:, None], 0.0)
    r = mxq(f64(wr), 0, "e4m3").T @ mxq(h, 0, "e4m3")
    d = r + f64(br)[:, None] - g
    return np.square(d)

@@ -1,0 +1,315 @@
+from contextlib import ExitStack
+
+import concourse.mybir as mybir
+from concourse.masks import make_identity
+
+K, C, H, N, T, S = 1024, 512, 1024, 256, 2048, 1024
+FLOPS = 2 * S * (K * H + C * H + H * N)
+
+F32 = mybir.dt.float32
+BF16 = mybir.dt.bfloat16
+I32 = mybir.dt.int32
+U32 = mybir.dt.uint32
+U16 = mybir.dt.uint16
+U8 = mybir.dt.uint8
+FP8X4 = mybir.dt.float8_e4m3fn_x4
+FP4X4 = mybir.dt.float4_e2m1fn_x4
+ALU = mybir.AluOpType
+ACT = mybir.ActivationFunctionType
+
+P = 128
+PACK = 4
+PASS = P * PACK
+HALF = 512
+LIST_COLS = HALF // 16
+PAIRED = ()
+
+
+def tile_list_replay_return_error_kernel(
+    tc, tab_words, tab_scales, tab2_words, tab2_scales, offs, offs2, wa, wb_words, wb_scales, bh, wr, br, gT, out
+):
+    nc = tc.nc
+    with ExitStack() as ctx:
+        keep = ctx.enter_context(tc.tile_pool(name="keep", bufs=1))
+        psum = ctx.enter_context(tc.psum_pool(name="psum", bufs=8))
+
+        def held(name, shape, dtype):
+            return keep.tile(shape, dtype, name=name, align_bytes=64)
+
+        idx = keep.tile([P, S // 16], U16, name="idx")
+        idx2 = keep.tile([P, S // 16], U16, name="idx2")
+        state_win = [held("state_win%d" % a, [P, T], I32) for a in range(2)]
+        action_win = held("action_win", [P, T], I32)
+        state_scale_win = held("state_scale_win", [P, T // 4], I32)
+        action_scale_win = held("action_scale_win", [P, T // 4], I32)
+        target_win = [held("target_win%d" % c, [P, T], F32) for c in range(2)]
+        state_codes = [held("state_codes%d" % a, [P, S], U32) for a in range(2)]
+        action_codes = held("action_codes", [P, S], U32)
+        state_scale = held("state_scale", [P, S], U8)
+        action_scale = held("action_scale", [P, S], U8)
+        target = [held("target%d" % c, [P, S], F32) for c in range(2)]
+        wa_raw = {(g, a): held("wa_raw%d%d" % (g, a), [P, PACK, PASS], F32) for g in range(2) for a in range(2)}
+        wa_bf = {(g, a): held("wa_bf%d%d" % (g, a), [P, PASS * PACK], BF16) for g in range(2) for a in range(2)}
+        wa_codes = {(g, a): held("wa_codes%d%d" % (g, a), [P, PASS], U32) for g in range(2) for a in range(2)}
+        wa_scale = {(g, a): held("wa_scale%d%d" % (g, a), [P, PASS], U8) for g in range(2) for a in range(2)}
+        wb_raw = held("wb_raw", [P, H // 2], I32)
+        wb_scale_raw = held("wb_scale_raw", [P, H // 4], I32)
+        wb_codes = held("wb_codes", [P, 2 * H], U8)
+        wb_scale = held("wb_scale", [P, H], U8)
+        wr_raw = [held("wr_raw%d" % g, [P, PACK, N], F32) for g in range(2)]
+        wr_bf = [held("wr_bf%d" % g, [P, N * PACK], BF16) for g in range(2)]
+        wr_codes = [held("wr_codes%d" % g, [P, N], U32) for g in range(2)]
+        wr_scale = [held("wr_scale%d" % g, [P, N], U8) for g in range(2)]
+        h_rows = {(g, j): held("h_rows%d%d" % (g, j), [P, PACK, HALF], BF16) for g in range(2) for j in range(2)}
+        h_bf = {(g, j): held("h_bf%d%d" % (g, j), [P, HALF * PACK], BF16) for g in range(2) for j in range(2)}
+        h_codes = {(g, j): held("h_codes%d%d" % (g, j), [P, HALF], U32) for g in range(2) for j in range(2)}
+        h_scale = {(g, j): held("h_scale%d%d" % (g, j), [P, HALF], U8) for g in range(2) for j in range(2)}
+        diff = {(c, j): held("diff%d%d" % (c, j), [P, HALF], F32) for c in range(2) for j in range(2)}
+        result = {(c, j): held("result%d%d" % (c, j), [P, HALF], F32) for c in range(2) for j in range(2)}
+        identity = held("identity", [P, P], F32)
+        bias_rows = held("bias_rows", [P, P], F32)
+        bias = held("bias", [P, 16], F32)
+
+        nc.vector.memset(state_scale_win[:], 0)
+        nc.vector.memset(action_scale_win[:], 0)
+        nc.gpsimd.memset(wb_scale_raw[:], 0)
+        nc.gpsimd.memset(bias_rows[:], 0.0)
+
+        def load_words(window, words):
+            nc.sync.dma_start(out=window[:], in_=words.rearrange("p t i -> p (t i)").bitcast(I32))
+
+        def load_wa(g, a):
+            rows = wa[a * PASS : (a + 1) * PASS, g * PASS : (g + 1) * PASS]
+            nc.sync.dma_start(out=wa_raw[g, a][:], in_=rows.rearrange("(p j) c -> p j c", j=PACK))
+
+        def load_wr(g):
+            rows = wr[g * PASS : (g + 1) * PASS, :].rearrange("(q t i) n -> t q i n", t=PACK, i=8)
+            for t in range(PACK):
+                nc.sync.dma_start(out=wr_raw[g][:, t, :], in_=rows[t])
+
+        def load_state_scales(queue):
+            for quad in range(4):
+                queue.dma_start(
+                    out=state_scale_win[32 * quad : 32 * quad + 8, :],
+                    in_=tab_scales.bitcast(I32)[:, 4 * quad : 4 * quad + 4, :],
+                )
+
+        def load_scales(queue, plane, rows):
+            for quad in range(4):
+                queue.dma_start(
+                    out=plane[32 * quad : 32 * quad + 4, :], in_=rows.bitcast(I32)[0, 4 * quad : 4 * quad + 4, :]
+                )
+
+        def load_bias(queue):
+            for g in range(2):
+                queue.dma_start(
+                    out=bias_rows[PACK * g : PACK * (g + 1), :].rearrange("t (q i) -> t q i", i=8),
+                    in_=bh[g * PASS : (g + 1) * PASS].rearrange("(q t i) -> t q i", t=PACK, i=8),
+                )
+            queue.dma_start(out=bias_rows[8:10, :], in_=br.rearrange("(c p) -> c p", p=P))
+
+        load_state_scales(nc.scalar)
+        load_scales(nc.scalar, action_scale_win, tab2_scales)
+        nc.sync.dma_start(idx[:], offs)
+        load_words(state_win[0], tab_words[0])
+        load_wa(0, 0)
+        nc.sync.dma_start(idx2[:], offs2)
+        load_words(state_win[1], tab_words[1])
+        load_bias(nc.sync)
+        load_wa(0, 1)
+        load_scales(nc.sync, wb_scale_raw, wb_scales)
+        nc.sync.dma_start(out=wb_raw[:], in_=wb_words[0].bitcast(I32))
+        load_words(action_win, tab2_words[0])
+        nc.sync.dma_start(out=target_win[0][:], in_=gT[0:P, :])
+        load_wa(1, 0)
+        load_wa(1, 1)
+        load_wr(0)
+        nc.sync.dma_start(out=target_win[1][:], in_=gT[P : 2 * P, :])
+        load_wr(1)
+
+        make_identity(nc, identity[:])
+
+
+        def bias_transpose():
+            bank = psum.tile([P, HALF], F32, name="bank")
+            nc.tensor.transpose(bank[:, 0:P], bias_rows[:], identity[:])
+            nc.scalar.copy(out=bias[:], in_=bank[:, 0:16])
+
+        def gather(dst, window, offsets, j):
+            picks = offsets[:, j * LIST_COLS : (j + 1) * LIST_COLS]
+            nc.vector.tensor_copy(dst[:, j * HALF : (j + 1) * HALF], window.indirect(picks))
+
+        def cast(engine, dst, src):
+            if engine == "S":
+                nc.scalar.copy(out=dst, in_=src)
+            elif engine == "V":
+                nc.vector.tensor_copy(out=dst, in_=src)
+            else:
+                nc.gpsimd.tensor_copy(out=dst, in_=src)
+
+        def cast_wa(g, a, engines):
+            src = wa_raw[g, a][:].rearrange("p j (q t u i) -> p t q u j i", t=PACK, u=2, i=4)
+            dst = wa_bf[g, a][:].rearrange("p (t q u i j) -> p t q u j i", t=PACK, u=2, i=4, j=PACK)
+            for t in range(PACK):
+                cast(engines[t], dst[:, t], src[:, t])
+
+        def quantize(codes, scale, values):
+            nc.vector.quantize_mx(out=codes.bitcast(FP8X4), scales=scale, in_=values)
+
+        def quantize_wa(g, a):
+            for t in range(PACK):
+                cols = slice(t * P, (t + 1) * P)
+                quantize(wa_codes[g, a][:, cols], wa_scale[g, a][:, cols], wa_bf[g, a][:, t * PASS : (t + 1) * PASS])
+
+        def permute_wb():
+            nc.vector.tensor_copy(
+                out=wb_codes[:].bitcast(I32).rearrange("p (g t q w) -> p g q t w", g=2, t=PACK, w=4),
+                in_=wb_raw[:].rearrange("p (g q t w) -> p g q t w", g=2, t=PACK, w=4),
+            )
+            nc.vector.tensor_copy(
+                out=wb_scale[:].bitcast(I32).rearrange("p (g t q w) -> p g q t w", g=2, t=PACK, w=2),
+                in_=wb_scale_raw[:].rearrange("p (g q t w) -> p g q t w", g=2, t=PACK, w=2),
+            )
+
+        hid_banks = {}
+
+        def relu_out(g, j, t, lo, hi):
+            col = PACK * g + t
+            if (g, j) in PAIRED:
+                dst = h_rows[g, j][:].rearrange("p t n -> p (t n)").rearrange("p (u n e) -> p u e n", u=2, e=2)[:, t // 2, t % 2, lo:hi]
+            else:
+                dst = h_rows[g, j][:, t, lo:hi]
+            nc.scalar.activation(out=dst, in_=hid_banks[g, j, t][:, lo:hi], func=ACT.Relu, bias=bias[:, col : col + 1])
+
+        def hidden(g, j, slots, passes, width):
+            tokens = slice(j * HALF, (j + 1) * HALF)
+            for t in slots:
+                bank = psum.tile([P, HALF], F32, name="bank")
+                hid_banks[g, j, t] = bank
+                cols = slice(t * P, (t + 1) * P)
+                first = (PACK * g + t) * P
+                for n, a in enumerate(passes):
+                    if a < 2:
+                        nc.tensor.matmul_mx(
+                            out=bank[:],
+                            lhsT=wa_codes[g, a][:, cols].bitcast(FP8X4),
+                            lhsT_scale=wa_scale[g, a][:, cols],
+                            rhs=state_codes[a][:, tokens].bitcast(FP8X4),
+                            rhs_scale=state_scale[4 * a : P, tokens],
+                            start=(n == 0),
+                            stop=(n == 2),
+                        )
+                    else:
+                        nc.tensor.matmul_mx(
+                            out=bank[:],
+                            lhsT=wb_codes[:, 2 * first : 2 * (first + P)].bitcast(FP4X4),
+                            lhsT_scale=wb_scale[:, first : first + P],
+                            rhs=action_codes[:, tokens].bitcast(FP8X4),
+                            rhs_scale=action_scale[:, tokens],
+                            start=(n == 0),
+                            stop=(n == 2),
+                        )
+                relu_out(g, j, t, 0, width)
+
+        def interleave_h(engine, g, j, lo, hi):
+            if (g, j) in PAIRED:
+                src = h_rows[g, j][:].rearrange("p t n -> p (t n)").rearrange("p (u n e) -> p n u e", u=2, e=2)[:, lo:hi]
+                cast(engine, h_bf[g, j][:].rearrange("p (n u e) -> p n u e", u=2, e=2)[:, lo:hi], src)
+            else:
+                cast(
+                    engine,
+                    h_bf[g, j][:, PACK * lo : PACK * hi].rearrange("p (c i t) -> p c t i", i=4, t=PACK),
+                    h_rows[g, j][:, :, lo:hi].rearrange("p t (c i) -> p c t i", i=4),
+                )
+
+        def quantize_h(g, j, lo, hi):
+            quantize(h_codes[g, j][:, lo:hi], h_scale[g, j][:, lo:hi], h_bf[g, j][:, PACK * lo : PACK * hi])
+
+        def cast_wr(engine, g):
+            cast(
+                engine,
+                wr_bf[g][:].rearrange("p (c i t) -> p c t i", i=4, t=PACK),
+                wr_raw[g][:].rearrange("p t (c i) -> p c t i", i=4),
+            )
+
+        def returns(c, j, lo, hi, square_engine):
+            tokens = slice(j * HALF + lo, j * HALF + hi)
+            bank = psum.tile([P, HALF], F32, name="bank")
+            cols = slice(c * P, (c + 1) * P)
+            for g in range(2):
+                nc.tensor.matmul_mx(
+                    out=bank[:, 0 : hi - lo],
+                    lhsT=wr_codes[g][:, cols].bitcast(FP8X4),
+                    lhsT_scale=wr_scale[g][:, cols],
+                    rhs=h_codes[g, j][:, lo:hi].bitcast(FP8X4),
+                    rhs_scale=h_scale[g, j][:, lo:hi],
+                    start=(g == 0),
+                    stop=(g == 1),
+                )
+            d = diff[c, j][:, lo:hi]
+            nc.vector.scalar_tensor_tensor(
+                out=d, in0=bank[:, 0 : hi - lo], scalar=bias[:, 8 + c : 9 + c], in1=target[c][:, tokens],
+                op0=ALU.add, op1=ALU.subtract,
+            )
+            if square_engine == "S":
+                nc.scalar.activation(out=result[c, j][:, lo:hi], in_=d, func=ACT.Square)
+            elif square_engine == "V":
+                nc.vector.tensor_tensor(out=result[c, j][:, lo:hi], in0=d, in1=d, op=ALU.mult)
+            else:
+                nc.gpsimd.tensor_tensor(out=result[c, j][:, lo:hi], in0=d, in1=d, op=ALU.mult)
+            nc.sync.dma_start(out=out[c * P : (c + 1) * P, tokens], in_=result[c, j][:, lo:hi])
+
+        gather(state_scale, state_scale_win[:].bitcast(U8), idx, 0)
+        gather(state_scale, state_scale_win[:].bitcast(U8), idx, 1)
+        bias_transpose()
+        cast_wa(0, 0, "SSSS")
+        gather(state_codes[0], state_win[0][:].bitcast(U32), idx, 0)
+        gather(state_codes[0], state_win[0][:].bitcast(U32), idx, 1)
+        gather(action_scale, action_scale_win[:].bitcast(U8), idx2, 0)
+        gather(action_scale, action_scale_win[:].bitcast(U8), idx2, 1)
+        quantize_wa(0, 0)
+        gather(state_codes[1], state_win[1][:].bitcast(U32), idx, 0)
+        cast_wa(0, 1, "SSSS")
+        gather(state_codes[1], state_win[1][:].bitcast(U32), idx, 1)
+        permute_wb()
+        quantize_wa(0, 1)
+        gather(action_codes, action_win[:].bitcast(U32), idx2, 0)
+        hidden(0, 0, (0, 1), (0, 1, 2), 512)
+        hidden(0, 0, (2, 3), (0, 1, 2), 512)
+        gather(action_codes, action_win[:].bitcast(U32), idx2, 1)
+        cast_wa(1, 0, "SSSS")
+        gather(target[0], target_win[0][:], idx, 0)
+        gather(target[0], target_win[0][:], idx, 1)
+        hidden(0, 1, (0, 1), (0, 1, 2), 512)
+        hidden(0, 1, (2, 3), (0, 1, 2), 512)
+        interleave_h("V", 0, 0, 0, 512)
+        quantize_h(0, 0, 0, 512)
+        quantize_wa(1, 0)
+        cast_wa(1, 1, "SSSS")
+        interleave_h("V", 0, 1, 0, 512)
+        quantize_wa(1, 1)
+        quantize_h(0, 1, 0, 512)
+        cast_wr("V", 0)
+        quantize(wr_codes[0][:], wr_scale[0][:], wr_bf[0][:])
+        hidden(1, 0, (0, 1), (0, 2, 1), 512)
+        hidden(1, 0, (2, 3), (0, 2, 1), 512)
+        cast_wr("V", 1)
+        quantize(wr_codes[1][:], wr_scale[1][:], wr_bf[1][:])
+        gather(target[1], target_win[1][:], idx, 0)
+        interleave_h("V", 1, 0, 0, 512)
+        quantize_h(1, 0, 0, 512)
+        hidden(1, 1, (0, 1), (0, 2, 1), 256)
+        hidden(1, 1, (2, 3), (0, 2, 1), 256)
+        for t in range(PACK):
+            relu_out(1, 1, t, 256, 512)
+        gather(target[1], target_win[1][:], idx, 1)
+        returns(0, 0, 0, 512, "S")
+        returns(1, 0, 0, 512, "S")
+        interleave_h("V", 1, 1, 0, 256)
+        quantize_h(1, 1, 0, 256)
+        interleave_h("V", 1, 1, 256, 512)
+        returns(0, 1, 0, 256, "S")
+        returns(1, 1, 0, 256, "S")
+        quantize_h(1, 1, 256, 512)
+        returns(0, 1, 256, 512, "S")
+        returns(1, 1, 256, 512, "V")

@@ -72,8 +72,8 @@ def tile_list_replay_return_error_kernel(
 
         nc.vector.memset(state_scale_win[:], 0)
         nc.vector.memset(action_scale_win[:], 0)
-        nc.gpsimd.memset(wb_scale_raw[:], 0)
-        nc.gpsimd.memset(bias_rows[:], 0.0)
+        nc.vector.memset(wb_scale_raw[:], 0)
+        nc.vector.memset(bias_rows[:], 0.0)
 
         def load_words(window, words):
             nc.sync.dma_start(out=window[:], in_=words.rearrange("p t i -> p (t i)").bitcast(I32))
@@ -108,22 +108,22 @@ def tile_list_replay_return_error_kernel(
                 )
             queue.dma_start(out=bias_rows[8:10, :], in_=br.rearrange("(c p) -> c p", p=P))
 
-        load_state_scales(nc.scalar)
-        load_scales(nc.scalar, action_scale_win, tab2_scales)
-        nc.sync.dma_start(idx[:], offs)
         load_words(state_win[0], tab_words[0])
-        load_wa(0, 0)
-        nc.sync.dma_start(idx2[:], offs2)
+        nc.sync.dma_start(idx[:], offs)
+        load_state_scales(nc.sync)
         load_words(state_win[1], tab_words[1])
-        load_bias(nc.sync)
-        load_wa(0, 1)
+        load_scales(nc.sync, action_scale_win, tab2_scales)
+        nc.sync.dma_start(idx2[:], offs2)
+        load_wa(0, 0)
         load_scales(nc.sync, wb_scale_raw, wb_scales)
+        load_wa(0, 1)
+        load_bias(nc.sync)
         nc.sync.dma_start(out=wb_raw[:], in_=wb_words[0].bitcast(I32))
+        load_wa(1, 0)
+        load_wr(0)
         load_words(action_win, tab2_words[0])
         nc.sync.dma_start(out=target_win[0][:], in_=gT[0:P, :])
-        load_wa(1, 0)
         load_wa(1, 1)
-        load_wr(0)
         nc.sync.dma_start(out=target_win[1][:], in_=gT[P : 2 * P, :])
         load_wr(1)
 
@@ -156,10 +156,12 @@ def tile_list_replay_return_error_kernel(
         def quantize(codes, scale, values):
             nc.vector.quantize_mx(out=codes.bitcast(FP8X4), scales=scale, in_=values)
 
-        def quantize_wa(g, a):
-            for t in range(PACK):
-                cols = slice(t * P, (t + 1) * P)
-                quantize(wa_codes[g, a][:, cols], wa_scale[g, a][:, cols], wa_bf[g, a][:, t * PASS : (t + 1) * PASS])
+        def quantize_wa(g, a, pieces):
+            width = PASS // pieces
+            for n in range(pieces):
+                cols = slice(n * width, (n + 1) * width)
+                values = wa_bf[g, a][:, PACK * n * width : PACK * (n + 1) * width]
+                quantize(wa_codes[g, a][:, cols], wa_scale[g, a][:, cols], values)
 
         def permute_wb():
             nc.vector.tensor_copy(
@@ -259,57 +261,57 @@ def tile_list_replay_return_error_kernel(
                 nc.gpsimd.tensor_tensor(out=result[c, j][:, lo:hi], in0=d, in1=d, op=ALU.mult)
             nc.sync.dma_start(out=out[c * P : (c + 1) * P, tokens], in_=result[c, j][:, lo:hi])
 
-        gather(state_scale, state_scale_win[:].bitcast(U8), idx, 0)
-        gather(state_scale, state_scale_win[:].bitcast(U8), idx, 1)
-        bias_transpose()
-        cast_wa(0, 0, "SSSS")
-        gather(state_codes[0], state_win[0][:].bitcast(U32), idx, 0)
-        gather(state_codes[0], state_win[0][:].bitcast(U32), idx, 1)
-        gather(action_scale, action_scale_win[:].bitcast(U8), idx2, 0)
-        gather(action_scale, action_scale_win[:].bitcast(U8), idx2, 1)
-        quantize_wa(0, 0)
-        gather(state_codes[1], state_win[1][:].bitcast(U32), idx, 0)
-        cast_wa(0, 1, "SSSS")
-        gather(state_codes[1], state_win[1][:].bitcast(U32), idx, 1)
-        permute_wb()
-        quantize_wa(0, 1)
-        gather(action_codes, action_win[:].bitcast(U32), idx2, 0)
-        hidden(0, 0, (0, 1), (0, 1, 2), 512)
-        hidden(0, 0, (2, 3), (0, 1, 2), 512)
         gather(action_codes, action_win[:].bitcast(U32), idx2, 1)
-        cast_wa(1, 0, "SSSS")
+        cast_wa(1, 0, "VVVS")
+        gather(state_scale, state_scale_win[:].bitcast(U8), idx, 1)
+        cast_wr("S", 0)
+        cast_wa(0, 0, "SSSS")
+        bias_transpose()
+        gather(state_codes[1], state_win[1][:].bitcast(U32), idx, 1)
+        gather(state_codes[1], state_win[1][:].bitcast(U32), idx, 0)
+        gather(action_scale, action_scale_win[:].bitcast(U8), idx2, 1)
+        cast_wa(1, 1, "VSVS")
+        quantize(wr_codes[0][:], wr_scale[0][:], wr_bf[0][:])
+        gather(target[1], target_win[1][:], idx, 0)
+        quantize_wa(0, 0, 1)
+        cast_wa(0, 1, "SVSS")
+        quantize_wa(0, 1, 2)
         gather(target[0], target_win[0][:], idx, 0)
-        gather(target[0], target_win[0][:], idx, 1)
+        gather(action_scale, action_scale_win[:].bitcast(U8), idx2, 0)
+        gather(state_scale, state_scale_win[:].bitcast(U8), idx, 0)
+        quantize_wa(1, 0, 2)
+        cast_wr("S", 1)
+        gather(state_codes[0], state_win[0][:].bitcast(U32), idx, 1)
+        gather(state_codes[0], state_win[0][:].bitcast(U32), idx, 0)
+        permute_wb()
+        gather(action_codes, action_win[:].bitcast(U32), idx2, 0)
+        quantize_wa(1, 1, 2)
         hidden(0, 1, (0, 1), (0, 1, 2), 512)
+        quantize(wr_codes[1][:], wr_scale[1][:], wr_bf[1][:])
         hidden(0, 1, (2, 3), (0, 1, 2), 512)
+        interleave_h("V", 0, 1, 0, 512)
+        hidden(0, 0, (0, 1), (0, 2, 1), 512)
+        hidden(1, 0, (0, 1), (0, 1, 2), 512)
+        gather(target[0], target_win[0][:], idx, 1)
+        hidden(1, 0, (2, 3), (0, 1, 2), 512)
+        hidden(1, 1, (0, 1), (2, 0, 1), 256)
+        hidden(0, 0, (2, 3), (0, 2, 1), 512)
         interleave_h("V", 0, 0, 0, 512)
         quantize_h(0, 0, 0, 512)
-        quantize_wa(1, 0)
-        cast_wa(1, 1, "SSSS")
-        interleave_h("V", 0, 1, 0, 512)
-        quantize_wa(1, 1)
-        quantize_h(0, 1, 0, 512)
-        cast_wr("V", 0)
-        quantize(wr_codes[0][:], wr_scale[0][:], wr_bf[0][:])
-        hidden(1, 0, (0, 1), (0, 2, 1), 512)
-        hidden(1, 0, (2, 3), (0, 2, 1), 512)
-        cast_wr("V", 1)
-        quantize(wr_codes[1][:], wr_scale[1][:], wr_bf[1][:])
-        gather(target[1], target_win[1][:], idx, 0)
         interleave_h("V", 1, 0, 0, 512)
+        hidden(1, 1, (2, 3), (2, 0, 1), 256)
+        gather(target[1], target_win[1][:], idx, 1)
         quantize_h(1, 0, 0, 512)
-        hidden(1, 1, (0, 1), (0, 2, 1), 256)
-        hidden(1, 1, (2, 3), (0, 2, 1), 256)
+        interleave_h("V", 1, 1, 0, 256)
         for t in range(PACK):
             relu_out(1, 1, t, 256, 512)
-        gather(target[1], target_win[1][:], idx, 1)
-        returns(0, 0, 0, 512, "S")
-        returns(1, 0, 0, 512, "S")
-        interleave_h("V", 1, 1, 0, 256)
         quantize_h(1, 1, 0, 256)
         interleave_h("V", 1, 1, 256, 512)
-        returns(0, 1, 0, 256, "S")
-        returns(1, 1, 0, 256, "S")
+        returns(0, 0, 0, 512, "S")
+        returns(1, 0, 0, 512, "S")
         quantize_h(1, 1, 256, 512)
+        quantize_h(0, 1, 0, 512)
+        returns(1, 1, 0, 256, "S")
+        returns(0, 1, 0, 256, "S")
         returns(0, 1, 256, 512, "S")
-        returns(1, 1, 256, 512, "V")
+        returns(1, 1, 256, 512, "S")

@@ -67,8 +67,9 @@ def tile_list_replay_return_error_kernel(
         diff = {(c, j): held("diff%d%d" % (c, j), [P, HALF], F32) for c in range(2) for j in range(2)}
         result = {(c, j): held("result%d%d" % (c, j), [P, HALF], F32) for c in range(2) for j in range(2)}
         identity = held("identity", [P, P], F32)
-        bias_rows = held("bias_rows", [P, P], F32)
-        bias = held("bias", [P, 16], F32)
+        bias_rows = held("bias_rows", [P, PASS], F32)
+        bias_in = held("bias_in", [P, PASS], F32)
+        bias = held("bias", [P, PACK, 4], F32)
 
         nc.vector.memset(state_scale_win[:], 0)
         nc.vector.memset(action_scale_win[:], 0)
@@ -95,45 +96,46 @@ def tile_list_replay_return_error_kernel(
                 )
 
         def load_scales(queue, plane, rows):
-            for quad in range(4):
-                queue.dma_start(
-                    out=plane[32 * quad : 32 * quad + 4, :], in_=rows.bitcast(I32)[0, 4 * quad : 4 * quad + 4, :]
-                )
+            for r in range(4):
+                queue.dma_start(out=plane[r:P:32, :], in_=rows.bitcast(I32)[0, r:16:4, :])
 
         def load_bias(queue):
-            for g in range(2):
-                queue.dma_start(
-                    out=bias_rows[PACK * g : PACK * (g + 1), :].rearrange("t (q i) -> t q i", i=8),
-                    in_=bh[g * PASS : (g + 1) * PASS].rearrange("(q t i) -> t q i", t=PACK, i=8),
-                )
-            queue.dma_start(out=bias_rows[8:10, :], in_=br.rearrange("(c p) -> c p", p=P))
+            queue.dma_start(out=bias_in[0:2, :], in_=bh.rearrange("(g r) -> g r", g=2))
+            queue.dma_start(out=bias_rows[2:3, 0:N], in_=br.rearrange("(o n) -> o n", o=1))
 
         load_words(state_win[0], tab_words[0])
         nc.sync.dma_start(idx[:], offs)
         load_state_scales(nc.sync)
-        load_words(state_win[1], tab_words[1])
         load_scales(nc.sync, action_scale_win, tab2_scales)
-        nc.sync.dma_start(idx2[:], offs2)
         load_wa(0, 0)
-        load_scales(nc.sync, wb_scale_raw, wb_scales)
-        load_wa(0, 1)
+        nc.sync.dma_start(idx2[:], offs2)
+        load_words(action_win, tab2_words[0])
         load_bias(nc.sync)
         nc.sync.dma_start(out=wb_raw[:], in_=wb_words[0].bitcast(I32))
-        load_wa(1, 0)
-        load_wr(0)
-        load_words(action_win, tab2_words[0])
+        load_wa(0, 1)
+        load_scales(nc.sync, wb_scale_raw, wb_scales)
+        load_words(state_win[1], tab_words[1])
         nc.sync.dma_start(out=target_win[0][:], in_=gT[0:P, :])
         load_wa(1, 1)
+        load_wa(1, 0)
+        load_wr(0)
         nc.sync.dma_start(out=target_win[1][:], in_=gT[P : 2 * P, :])
         load_wr(1)
 
         make_identity(nc, identity[:])
 
 
+        def bias_permute():
+            nc.scalar.copy(
+                out=bias_rows[0:2, :].rearrange("g (t q i) -> g q t i", t=PACK, i=8),
+                in_=bias_in[0:2, :].rearrange("g (q t i) -> g q t i", t=PACK, i=8),
+            )
+
         def bias_transpose():
             bank = psum.tile([P, HALF], F32, name="bank")
-            nc.tensor.transpose(bank[:, 0:P], bias_rows[:], identity[:])
-            nc.scalar.copy(out=bias[:], in_=bank[:, 0:16])
+            for t in range(PACK):
+                nc.tensor.transpose(bank[:, t * P : (t + 1) * P], bias_rows[:, t * P : (t + 1) * P], identity[:])
+            nc.scalar.copy(out=bias[:], in_=bank[:].rearrange("p (t x) -> p t x", t=PACK)[:, :, 0:4])
 
         def gather(dst, window, offsets, j):
             picks = offsets[:, j * LIST_COLS : (j + 1) * LIST_COLS]
@@ -176,12 +178,11 @@ def tile_list_replay_return_error_kernel(
         hid_banks = {}
 
         def relu_out(g, j, t, lo, hi):
-            col = PACK * g + t
             if (g, j) in PAIRED:
                 dst = h_rows[g, j][:].rearrange("p t n -> p (t n)").rearrange("p (u n e) -> p u e n", u=2, e=2)[:, t // 2, t % 2, lo:hi]
             else:
                 dst = h_rows[g, j][:, t, lo:hi]
-            nc.scalar.activation(out=dst, in_=hid_banks[g, j, t][:, lo:hi], func=ACT.Relu, bias=bias[:, col : col + 1])
+            nc.scalar.activation(out=dst, in_=hid_banks[g, j, t][:, lo:hi], func=ACT.Relu, bias=bias[:, t, g : g + 1])
 
         def hidden(g, j, slots, passes, width):
             tokens = slice(j * HALF, (j + 1) * HALF)
@@ -250,7 +251,7 @@ def tile_list_replay_return_error_kernel(
                 )
             d = diff[c, j][:, lo:hi]
             nc.vector.scalar_tensor_tensor(
-                out=d, in0=bank[:, 0 : hi - lo], scalar=bias[:, 8 + c : 9 + c], in1=target[c][:, tokens],
+                out=d, in0=bank[:, 0 : hi - lo], scalar=bias[:, c, 2:3], in1=target[c][:, tokens],
                 op0=ALU.add, op1=ALU.subtract,
             )
             if square_engine == "S":
@@ -261,48 +262,50 @@ def tile_list_replay_return_error_kernel(
                 nc.gpsimd.tensor_tensor(out=result[c, j][:, lo:hi], in0=d, in1=d, op=ALU.mult)
             nc.sync.dma_start(out=out[c * P : (c + 1) * P, tokens], in_=result[c, j][:, lo:hi])
 
-        gather(action_codes, action_win[:].bitcast(U32), idx2, 1)
-        cast_wa(1, 0, "VVVS")
-        gather(state_scale, state_scale_win[:].bitcast(U8), idx, 1)
-        cast_wr("S", 0)
-        cast_wa(0, 0, "SSSS")
-        bias_transpose()
-        gather(state_codes[1], state_win[1][:].bitcast(U32), idx, 1)
-        gather(state_codes[1], state_win[1][:].bitcast(U32), idx, 0)
-        gather(action_scale, action_scale_win[:].bitcast(U8), idx2, 1)
-        cast_wa(1, 1, "VSVS")
-        quantize(wr_codes[0][:], wr_scale[0][:], wr_bf[0][:])
-        gather(target[1], target_win[1][:], idx, 0)
-        quantize_wa(0, 0, 1)
-        cast_wa(0, 1, "SVSS")
-        quantize_wa(0, 1, 2)
-        gather(target[0], target_win[0][:], idx, 0)
-        gather(action_scale, action_scale_win[:].bitcast(U8), idx2, 0)
-        gather(state_scale, state_scale_win[:].bitcast(U8), idx, 0)
-        quantize_wa(1, 0, 2)
-        cast_wr("S", 1)
-        gather(state_codes[0], state_win[0][:].bitcast(U32), idx, 1)
         gather(state_codes[0], state_win[0][:].bitcast(U32), idx, 0)
-        permute_wb()
+        gather(state_codes[0], state_win[0][:].bitcast(U32), idx, 1)
+        gather(state_scale, state_scale_win[:].bitcast(U8), idx, 0)
+        gather(state_scale, state_scale_win[:].bitcast(U8), idx, 1)
+        cast_wa(0, 0, "SSSS")
+        gather(action_scale, action_scale_win[:].bitcast(U8), idx2, 0)
+        gather(action_scale, action_scale_win[:].bitcast(U8), idx2, 1)
+        quantize_wa(0, 0, 4)
+        bias_permute()
+        bias_transpose()
         gather(action_codes, action_win[:].bitcast(U32), idx2, 0)
-        quantize_wa(1, 1, 2)
-        hidden(0, 1, (0, 1), (0, 1, 2), 512)
-        quantize(wr_codes[1][:], wr_scale[1][:], wr_bf[1][:])
-        hidden(0, 1, (2, 3), (0, 1, 2), 512)
-        interleave_h("V", 0, 1, 0, 512)
+        gather(action_codes, action_win[:].bitcast(U32), idx2, 1)
+        cast_wa(0, 1, "VSSV")
+        quantize_wa(0, 1, 4)
+        permute_wb()
+        gather(state_codes[1], state_win[1][:].bitcast(U32), idx, 0)
+        gather(state_codes[1], state_win[1][:].bitcast(U32), idx, 1)
         hidden(0, 0, (0, 1), (0, 2, 1), 512)
-        hidden(1, 0, (0, 1), (0, 1, 2), 512)
-        gather(target[0], target_win[0][:], idx, 1)
-        hidden(1, 0, (2, 3), (0, 1, 2), 512)
-        hidden(1, 1, (0, 1), (2, 0, 1), 256)
         hidden(0, 0, (2, 3), (0, 2, 1), 512)
+        hidden(0, 1, (0, 1), (0, 1, 2), 512)
+        hidden(0, 1, (2, 3), (0, 1, 2), 512)
+        gather(target[0], target_win[0][:], idx, 0)
+        gather(target[0], target_win[0][:], idx, 1)
+        cast_wa(1, 1, "VVVS")
         interleave_h("V", 0, 0, 0, 512)
+        quantize_wa(1, 1, 1)
+        cast_wa(1, 0, "SSVS")
+        interleave_h("V", 0, 1, 0, 512)
+        quantize_wa(1, 0, 2)
         quantize_h(0, 0, 0, 512)
-        interleave_h("V", 1, 0, 0, 512)
+        quantize_h(0, 1, 0, 512)
+        cast_wr("S", 0)
+        quantize(wr_codes[0][:], wr_scale[0][:], wr_bf[0][:])
+        hidden(1, 0, (0, 1), (2, 1, 0), 512)
+        hidden(1, 0, (2, 3), (2, 1, 0), 512)
+        hidden(1, 1, (0, 1), (2, 0, 1), 256)
         hidden(1, 1, (2, 3), (2, 0, 1), 256)
+        gather(target[1], target_win[1][:], idx, 0)
         gather(target[1], target_win[1][:], idx, 1)
-        quantize_h(1, 0, 0, 512)
+        interleave_h("V", 1, 0, 0, 512)
+        cast_wr("S", 1)
         interleave_h("V", 1, 1, 0, 256)
+        quantize_h(1, 0, 0, 512)
+        quantize(wr_codes[1][:], wr_scale[1][:], wr_bf[1][:])
         for t in range(PACK):
             relu_out(1, 1, t, 256, 512)
         quantize_h(1, 1, 0, 256)
@@ -310,8 +313,7 @@ def tile_list_replay_return_error_kernel(
         returns(0, 0, 0, 512, "S")
         returns(1, 0, 0, 512, "S")
         quantize_h(1, 1, 256, 512)
-        quantize_h(0, 1, 0, 512)
-        returns(1, 1, 0, 256, "S")
         returns(0, 1, 0, 256, "S")
+        returns(1, 1, 0, 256, "S")
         returns(0, 1, 256, 512, "S")
         returns(1, 1, 256, 512, "S")

@@ -107,20 +107,20 @@ def tile_list_replay_return_error_kernel(
         nc.sync.dma_start(idx[:], offs)
         load_state_scales(nc.sync)
         load_scales(nc.sync, action_scale_win, tab2_scales)
-        load_wa(0, 0)
         nc.sync.dma_start(idx2[:], offs2)
+        load_wa(0, 0)
+        load_scales(nc.sync, wb_scale_raw, wb_scales)
+        nc.sync.dma_start(out=wb_raw[:], in_=wb_words[0].bitcast(I32))
         load_words(action_win, tab2_words[0])
         load_bias(nc.sync)
-        nc.sync.dma_start(out=wb_raw[:], in_=wb_words[0].bitcast(I32))
         load_wa(0, 1)
-        load_scales(nc.sync, wb_scale_raw, wb_scales)
         load_words(state_win[1], tab_words[1])
         nc.sync.dma_start(out=target_win[0][:], in_=gT[0:P, :])
         load_wa(1, 1)
-        load_wa(1, 0)
-        load_wr(0)
-        nc.sync.dma_start(out=target_win[1][:], in_=gT[P : 2 * P, :])
         load_wr(1)
+        load_wr(0)
+        load_wa(1, 0)
+        nc.sync.dma_start(out=target_win[1][:], in_=gT[P : 2 * P, :])
 
         make_identity(nc, identity[:])
 
@@ -266,48 +266,48 @@ def tile_list_replay_return_error_kernel(
         gather(state_codes[0], state_win[0][:].bitcast(U32), idx, 1)
         gather(state_scale, state_scale_win[:].bitcast(U8), idx, 0)
         gather(state_scale, state_scale_win[:].bitcast(U8), idx, 1)
-        cast_wa(0, 0, "SSSS")
         gather(action_scale, action_scale_win[:].bitcast(U8), idx2, 0)
         gather(action_scale, action_scale_win[:].bitcast(U8), idx2, 1)
-        quantize_wa(0, 0, 4)
+        cast_wa(0, 0, "SSSS")
+        quantize_wa(0, 0, 2)
         bias_permute()
         bias_transpose()
+        permute_wb()
         gather(action_codes, action_win[:].bitcast(U32), idx2, 0)
         gather(action_codes, action_win[:].bitcast(U32), idx2, 1)
-        cast_wa(0, 1, "VSSV")
+        cast_wa(0, 1, "VSSS")
         quantize_wa(0, 1, 4)
-        permute_wb()
         gather(state_codes[1], state_win[1][:].bitcast(U32), idx, 0)
         gather(state_codes[1], state_win[1][:].bitcast(U32), idx, 1)
         hidden(0, 0, (0, 1), (0, 2, 1), 512)
         hidden(0, 0, (2, 3), (0, 2, 1), 512)
-        hidden(0, 1, (0, 1), (0, 1, 2), 512)
-        hidden(0, 1, (2, 3), (0, 1, 2), 512)
+        hidden(0, 1, (0, 1), (2, 1, 0), 512)
+        hidden(0, 1, (2, 3), (2, 1, 0), 512)
         gather(target[0], target_win[0][:], idx, 0)
         gather(target[0], target_win[0][:], idx, 1)
-        cast_wa(1, 1, "VVVS")
+        cast_wa(1, 1, "VVVV")
         interleave_h("V", 0, 0, 0, 512)
-        quantize_wa(1, 1, 1)
-        cast_wa(1, 0, "SSVS")
         interleave_h("V", 0, 1, 0, 512)
-        quantize_wa(1, 0, 2)
+        quantize_wa(1, 1, 1)
         quantize_h(0, 0, 0, 512)
         quantize_h(0, 1, 0, 512)
+        cast_wa(1, 0, "VSSS")
+        quantize_wa(1, 0, 4)
+        cast_wr("S", 1)
         cast_wr("S", 0)
+        quantize(wr_codes[1][:], wr_scale[1][:], wr_bf[1][:])
         quantize(wr_codes[0][:], wr_scale[0][:], wr_bf[0][:])
+        gather(target[1], target_win[1][:], idx, 0)
+        gather(target[1], target_win[1][:], idx, 1)
         hidden(1, 0, (0, 1), (2, 1, 0), 512)
         hidden(1, 0, (2, 3), (2, 1, 0), 512)
         hidden(1, 1, (0, 1), (2, 0, 1), 256)
         hidden(1, 1, (2, 3), (2, 0, 1), 256)
-        gather(target[1], target_win[1][:], idx, 0)
-        gather(target[1], target_win[1][:], idx, 1)
         interleave_h("V", 1, 0, 0, 512)
-        cast_wr("S", 1)
         interleave_h("V", 1, 1, 0, 256)
-        quantize_h(1, 0, 0, 512)
-        quantize(wr_codes[1][:], wr_scale[1][:], wr_bf[1][:])
         for t in range(PACK):
             relu_out(1, 1, t, 256, 512)
+        quantize_h(1, 0, 0, 512)
         quantize_h(1, 1, 0, 256)
         interleave_h("V", 1, 1, 256, 512)
         returns(0, 0, 0, 512, "S")
@@ -316,4 +316,4 @@ def tile_list_replay_return_error_kernel(
         returns(0, 1, 0, 256, "S")
         returns(1, 1, 0, 256, "S")
         returns(0, 1, 256, 512, "S")
-        returns(1, 1, 256, 512, "S")
+        returns(1, 1, 256, 512, "V")

from contextlib import ExitStack

import concourse.mybir as mybir
from concourse.masks import make_identity

K, C, H, N, T, S = 1024, 512, 1024, 256, 2048, 1024
FLOPS = 2 * S * (K * H + C * H + H * N)

F32 = mybir.dt.float32
BF16 = mybir.dt.bfloat16
I32 = mybir.dt.int32
U32 = mybir.dt.uint32
U16 = mybir.dt.uint16
U8 = mybir.dt.uint8
FP8X4 = mybir.dt.float8_e4m3fn_x4
FP4X4 = mybir.dt.float4_e2m1fn_x4
ALU = mybir.AluOpType
ACT = mybir.ActivationFunctionType

P = 128
PACK = 4
PASS = P * PACK
HALF = 512
LIST_COLS = HALF // 16
PAIRED = ()


def tile_list_replay_return_error_kernel(
    tc, tab_words, tab_scales, tab2_words, tab2_scales, offs, offs2, wa, wb_words, wb_scales, bh, wr, br, gT, out
):
    nc = tc.nc
    with ExitStack() as ctx:
        keep = ctx.enter_context(tc.tile_pool(name="keep", bufs=1))
        psum = ctx.enter_context(tc.psum_pool(name="psum", bufs=8))

        def held(name, shape, dtype):
            return keep.tile(shape, dtype, name=name, align_bytes=64)

        idx = keep.tile([P, S // 16], U16, name="idx")
        idx2 = keep.tile([P, S // 16], U16, name="idx2")
        state_win = [held("state_win%d" % a, [P, T], I32) for a in range(2)]
        action_win = held("action_win", [P, T], I32)
        state_scale_win = held("state_scale_win", [P, T // 4], I32)
        action_scale_win = held("action_scale_win", [P, T // 4], I32)
        target_win = [held("target_win%d" % c, [P, T], F32) for c in range(2)]
        state_codes = [held("state_codes%d" % a, [P, S], U32) for a in range(2)]
        action_codes = held("action_codes", [P, S], U32)
        state_scale = held("state_scale", [P, S], U8)
        action_scale = held("action_scale", [P, S], U8)
        target = [held("target%d" % c, [P, S], F32) for c in range(2)]
        wa_raw = {(g, a): held("wa_raw%d%d" % (g, a), [P, PACK, PASS], F32) for g in range(2) for a in range(2)}
        wa_bf = {(g, a): held("wa_bf%d%d" % (g, a), [P, PASS * PACK], BF16) for g in range(2) for a in range(2)}
        wa_codes = {(g, a): held("wa_codes%d%d" % (g, a), [P, PASS], U32) for g in range(2) for a in range(2)}
        wa_scale = {(g, a): held("wa_scale%d%d" % (g, a), [P, PASS], U8) for g in range(2) for a in range(2)}
        wb_raw = held("wb_raw", [P, H // 2], I32)
        wb_scale_raw = held("wb_scale_raw", [P, H // 4], I32)
        wb_codes = held("wb_codes", [P, 2 * H], U8)
        wb_scale = held("wb_scale", [P, H], U8)
        wr_raw = [held("wr_raw%d" % g, [P, PACK, N], F32) for g in range(2)]
        wr_bf = [held("wr_bf%d" % g, [P, N * PACK], BF16) for g in range(2)]
        wr_codes = [held("wr_codes%d" % g, [P, N], U32) for g in range(2)]
        wr_scale = [held("wr_scale%d" % g, [P, N], U8) for g in range(2)]
        h_rows = {(g, j): held("h_rows%d%d" % (g, j), [P, PACK, HALF], BF16) for g in range(2) for j in range(2)}
        h_bf = {(g, j): held("h_bf%d%d" % (g, j), [P, HALF * PACK], BF16) for g in range(2) for j in range(2)}
        h_codes = {(g, j): held("h_codes%d%d" % (g, j), [P, HALF], U32) for g in range(2) for j in range(2)}
        h_scale = {(g, j): held("h_scale%d%d" % (g, j), [P, HALF], U8) for g in range(2) for j in range(2)}
        diff = {(c, j): held("diff%d%d" % (c, j), [P, HALF], F32) for c in range(2) for j in range(2)}
        result = {(c, j): held("result%d%d" % (c, j), [P, HALF], F32) for c in range(2) for j in range(2)}
        identity = held("identity", [P, P], F32)
        bias_rows = held("bias_rows", [P, PASS], F32)
        bias_in = held("bias_in", [P, PASS], F32)
        bias = held("bias", [P, PACK, 4], F32)

        nc.vector.memset(state_scale_win[:], 0)
        nc.vector.memset(action_scale_win[:], 0)
        nc.vector.memset(wb_scale_raw[:], 0)
        nc.vector.memset(bias_rows[:], 0.0)

        def load_words(window, words):
            nc.sync.dma_start(out=window[:], in_=words.rearrange("p t i -> p (t i)").bitcast(I32))

        def load_wa(g, a):
            rows = wa[a * PASS : (a + 1) * PASS, g * PASS : (g + 1) * PASS]
            nc.sync.dma_start(out=wa_raw[g, a][:], in_=rows.rearrange("(p j) c -> p j c", j=PACK))

        def load_wr(g):
            rows = wr[g * PASS : (g + 1) * PASS, :].rearrange("(q t i) n -> t q i n", t=PACK, i=8)
            for t in range(PACK):
                nc.sync.dma_start(out=wr_raw[g][:, t, :], in_=rows[t])

        def load_state_scales(queue):
            for quad in range(4):
                queue.dma_start(
                    out=state_scale_win[32 * quad : 32 * quad + 8, :],
                    in_=tab_scales.bitcast(I32)[:, 4 * quad : 4 * quad + 4, :],
                )

        def load_scales(queue, plane, rows):
            for r in range(4):
                queue.dma_start(out=plane[r:P:32, :], in_=rows.bitcast(I32)[0, r:16:4, :])

        def load_bias(queue):
            queue.dma_start(out=bias_in[0:2, :], in_=bh.rearrange("(g r) -> g r", g=2))
            queue.dma_start(out=bias_rows[2:3, 0:N], in_=br.rearrange("(o n) -> o n", o=1))

        load_words(state_win[0], tab_words[0])
        nc.sync.dma_start(idx[:], offs)
        load_state_scales(nc.sync)
        load_scales(nc.sync, action_scale_win, tab2_scales)
        nc.sync.dma_start(idx2[:], offs2)
        load_wa(0, 0)
        load_scales(nc.sync, wb_scale_raw, wb_scales)
        nc.sync.dma_start(out=wb_raw[:], in_=wb_words[0].bitcast(I32))
        load_words(action_win, tab2_words[0])
        load_bias(nc.sync)
        load_wa(0, 1)
        load_words(state_win[1], tab_words[1])
        nc.sync.dma_start(out=target_win[0][:], in_=gT[0:P, :])
        load_wa(1, 1)
        load_wr(1)
        load_wr(0)
        load_wa(1, 0)
        nc.sync.dma_start(out=target_win[1][:], in_=gT[P : 2 * P, :])

        make_identity(nc, identity[:])


        def bias_permute():
            nc.scalar.copy(
                out=bias_rows[0:2, :].rearrange("g (t q i) -> g q t i", t=PACK, i=8),
                in_=bias_in[0:2, :].rearrange("g (q t i) -> g q t i", t=PACK, i=8),
            )

        def bias_transpose():
            bank = psum.tile([P, HALF], F32, name="bank")
            for t in range(PACK):
                nc.tensor.transpose(bank[:, t * P : (t + 1) * P], bias_rows[:, t * P : (t + 1) * P], identity[:])
            nc.scalar.copy(out=bias[:], in_=bank[:].rearrange("p (t x) -> p t x", t=PACK)[:, :, 0:4])

        def gather(dst, window, offsets, j):
            picks = offsets[:, j * LIST_COLS : (j + 1) * LIST_COLS]
            nc.vector.tensor_copy(dst[:, j * HALF : (j + 1) * HALF], window.indirect(picks))

        def cast(engine, dst, src):
            if engine == "S":
                nc.scalar.copy(out=dst, in_=src)
            elif engine == "V":
                nc.vector.tensor_copy(out=dst, in_=src)
            else:
                nc.gpsimd.tensor_copy(out=dst, in_=src)

        def cast_wa(g, a, engines):
            src = wa_raw[g, a][:].rearrange("p j (q t u i) -> p t q u j i", t=PACK, u=2, i=4)
            dst = wa_bf[g, a][:].rearrange("p (t q u i j) -> p t q u j i", t=PACK, u=2, i=4, j=PACK)
            for t in range(PACK):
                cast(engines[t], dst[:, t], src[:, t])

        def quantize(codes, scale, values):
            nc.vector.quantize_mx(out=codes.bitcast(FP8X4), scales=scale, in_=values)

        def quantize_wa(g, a, pieces):
            width = PASS // pieces
            for n in range(pieces):
                cols = slice(n * width, (n + 1) * width)
                values = wa_bf[g, a][:, PACK * n * width : PACK * (n + 1) * width]
                quantize(wa_codes[g, a][:, cols], wa_scale[g, a][:, cols], values)

        def permute_wb():
            nc.vector.tensor_copy(
                out=wb_codes[:].bitcast(I32).rearrange("p (g t q w) -> p g q t w", g=2, t=PACK, w=4),
                in_=wb_raw[:].rearrange("p (g q t w) -> p g q t w", g=2, t=PACK, w=4),
            )
            nc.vector.tensor_copy(
                out=wb_scale[:].bitcast(I32).rearrange("p (g t q w) -> p g q t w", g=2, t=PACK, w=2),
                in_=wb_scale_raw[:].rearrange("p (g q t w) -> p g q t w", g=2, t=PACK, w=2),
            )

        hid_banks = {}

        def relu_out(g, j, t, lo, hi):
            if (g, j) in PAIRED:
                dst = h_rows[g, j][:].rearrange("p t n -> p (t n)").rearrange("p (u n e) -> p u e n", u=2, e=2)[:, t // 2, t % 2, lo:hi]
            else:
                dst = h_rows[g, j][:, t, lo:hi]
            nc.scalar.activation(out=dst, in_=hid_banks[g, j, t][:, lo:hi], func=ACT.Relu, bias=bias[:, t, g : g + 1])

        def hidden(g, j, slots, passes, width):
            tokens = slice(j * HALF, (j + 1) * HALF)
            for t in slots:
                bank = psum.tile([P, HALF], F32, name="bank")
                hid_banks[g, j, t] = bank
                cols = slice(t * P, (t + 1) * P)
                first = (PACK * g + t) * P
                for n, a in enumerate(passes):
                    if a < 2:
                        nc.tensor.matmul_mx(
                            out=bank[:],
                            lhsT=wa_codes[g, a][:, cols].bitcast(FP8X4),
                            lhsT_scale=wa_scale[g, a][:, cols],
                            rhs=state_codes[a][:, tokens].bitcast(FP8X4),
                            rhs_scale=state_scale[4 * a : P, tokens],
                            start=(n == 0),
                            stop=(n == 2),
                        )
                    else:
                        nc.tensor.matmul_mx(
                            out=bank[:],
                            lhsT=wb_codes[:, 2 * first : 2 * (first + P)].bitcast(FP4X4),
                            lhsT_scale=wb_scale[:, first : first + P],
                            rhs=action_codes[:, tokens].bitcast(FP8X4),
                            rhs_scale=action_scale[:, tokens],
                            start=(n == 0),
                            stop=(n == 2),
                        )
                relu_out(g, j, t, 0, width)

        def interleave_h(engine, g, j, lo, hi):
            if (g, j) in PAIRED:
                src = h_rows[g, j][:].rearrange("p t n -> p (t n)").rearrange("p (u n e) -> p n u e", u=2, e=2)[:, lo:hi]
                cast(engine, h_bf[g, j][:].rearrange("p (n u e) -> p n u e", u=2, e=2)[:, lo:hi], src)
            else:
                cast(
                    engine,
                    h_bf[g, j][:, PACK * lo : PACK * hi].rearrange("p (c i t) -> p c t i", i=4, t=PACK),
                    h_rows[g, j][:, :, lo:hi].rearrange("p t (c i) -> p c t i", i=4),
                )

        def quantize_h(g, j, lo, hi):
            quantize(h_codes[g, j][:, lo:hi], h_scale[g, j][:, lo:hi], h_bf[g, j][:, PACK * lo : PACK * hi])

        def cast_wr(engine, g):
            cast(
                engine,
                wr_bf[g][:].rearrange("p (c i t) -> p c t i", i=4, t=PACK),
                wr_raw[g][:].rearrange("p t (c i) -> p c t i", i=4),
            )

        def returns(c, j, lo, hi, square_engine):
            tokens = slice(j * HALF + lo, j * HALF + hi)
            bank = psum.tile([P, HALF], F32, name="bank")
            cols = slice(c * P, (c + 1) * P)
            for g in range(2):
                nc.tensor.matmul_mx(
                    out=bank[:, 0 : hi - lo],
                    lhsT=wr_codes[g][:, cols].bitcast(FP8X4),
                    lhsT_scale=wr_scale[g][:, cols],
                    rhs=h_codes[g, j][:, lo:hi].bitcast(FP8X4),
                    rhs_scale=h_scale[g, j][:, lo:hi],
                    start=(g == 0),
                    stop=(g == 1),
                )
            d = diff[c, j][:, lo:hi]
            nc.vector.scalar_tensor_tensor(
                out=d, in0=bank[:, 0 : hi - lo], scalar=bias[:, c, 2:3], in1=target[c][:, tokens],
                op0=ALU.add, op1=ALU.subtract,
            )
            if square_engine == "S":
                nc.scalar.activation(out=result[c, j][:, lo:hi], in_=d, func=ACT.Square)
            elif square_engine == "V":
                nc.vector.tensor_tensor(out=result[c, j][:, lo:hi], in0=d, in1=d, op=ALU.mult)
            else:
                nc.gpsimd.tensor_tensor(out=result[c, j][:, lo:hi], in0=d, in1=d, op=ALU.mult)
            nc.sync.dma_start(out=out[c * P : (c + 1) * P, tokens], in_=result[c, j][:, lo:hi])

        gather(state_codes[0], state_win[0][:].bitcast(U32), idx, 0)
        gather(state_codes[0], state_win[0][:].bitcast(U32), idx, 1)
        gather(state_scale, state_scale_win[:].bitcast(U8), idx, 0)
        gather(state_scale, state_scale_win[:].bitcast(U8), idx, 1)
        gather(action_scale, action_scale_win[:].bitcast(U8), idx2, 0)
        gather(action_scale, action_scale_win[:].bitcast(U8), idx2, 1)
        cast_wa(0, 0, "SSSS")
        quantize_wa(0, 0, 2)
        bias_permute()
        bias_transpose()
        permute_wb()
        gather(action_codes, action_win[:].bitcast(U32), idx2, 0)
        gather(action_codes, action_win[:].bitcast(U32), idx2, 1)
        cast_wa(0, 1, "VSSS")
        quantize_wa(0, 1, 4)
        gather(state_codes[1], state_win[1][:].bitcast(U32), idx, 0)
        gather(state_codes[1], state_win[1][:].bitcast(U32), idx, 1)
        hidden(0, 0, (0, 1), (0, 2, 1), 512)
        hidden(0, 0, (2, 3), (0, 2, 1), 512)
        hidden(0, 1, (0, 1), (2, 1, 0), 512)
        hidden(0, 1, (2, 3), (2, 1, 0), 512)
        gather(target[0], target_win[0][:], idx, 0)
        gather(target[0], target_win[0][:], idx, 1)
        cast_wa(1, 1, "VVVV")
        interleave_h("V", 0, 0, 0, 512)
        interleave_h("V", 0, 1, 0, 512)
        quantize_wa(1, 1, 1)
        quantize_h(0, 0, 0, 512)
        quantize_h(0, 1, 0, 512)
        cast_wa(1, 0, "VSSS")
        quantize_wa(1, 0, 4)
        cast_wr("S", 1)
        cast_wr("S", 0)
        quantize(wr_codes[1][:], wr_scale[1][:], wr_bf[1][:])
        quantize(wr_codes[0][:], wr_scale[0][:], wr_bf[0][:])
        gather(target[1], target_win[1][:], idx, 0)
        gather(target[1], target_win[1][:], idx, 1)
        hidden(1, 0, (0, 1), (2, 1, 0), 512)
        hidden(1, 0, (2, 3), (2, 1, 0), 512)
        hidden(1, 1, (0, 1), (2, 0, 1), 256)
        hidden(1, 1, (2, 3), (2, 0, 1), 256)
        interleave_h("V", 1, 0, 0, 512)
        interleave_h("V", 1, 1, 0, 256)
        for t in range(PACK):
            relu_out(1, 1, t, 256, 512)
        quantize_h(1, 0, 0, 512)
        quantize_h(1, 1, 0, 256)
        interleave_h("V", 1, 1, 256, 512)
        returns(0, 0, 0, 512, "S")
        returns(1, 0, 0, 512, "S")
        quantize_h(1, 1, 256, 512)
        returns(0, 1, 0, 256, "S")
        returns(1, 1, 0, 256, "S")
        returns(0, 1, 256, 512, "S")
        returns(1, 1, 256, 512, "V")
